import numpy as np
import ml_dtypes


def mxq(x, axis, fmt="e4m3"):
    dtype, down = {"e4m3": (ml_dtypes.float8_e4m3fn, 7), "e5m2": (ml_dtypes.float8_e5m2, 14)}[fmt]
    v = np.moveaxis(np.asarray(x, np.float32).astype(ml_dtypes.bfloat16).astype(np.float64), axis, -1)
    blocks = v.reshape(v.shape[:-1] + (-1, 32))
    amax = np.abs(blocks).max(-1, keepdims=True)
    byte = np.maximum(np.where(amax > 0, np.frexp(amax)[1] - 1 + 127, 0) - down, 1)
    scale = np.exp2(byte - 127.0)
    codes = (blocks / scale).astype(np.float32).astype(dtype).astype(np.float64)
    return np.moveaxis((codes * scale).reshape(v.shape), -1, axis)


WIDE = False


def mx_kscale(k):
    if not WIDE:
        return np.ones(k)
    levels = np.array([10, -10, 5, -5, 0])
    if k % 512:
        return np.exp2(np.random.permutation(np.resize(levels, k // 32))).repeat(32)
    a = np.empty((k // 512, 16))
    for p in range(k // 512):
        a[p, :8] = np.random.permutation(np.resize(levels, 8))
        for g in range(8):
            far = levels[np.abs(levels - a[p, g]) >= 10]
            a[p, g + 8] = far[np.random.randint(len(far))]
    return np.exp2(a.ravel()).repeat(32)


def f64(x):
    return np.asarray(x).astype(np.float64)


def striped(idx):
    return np.tile(idx.reshape(-1, 16).T, (8, 1)).astype(np.uint16)


def unstriped(offs):
    return offs[:16].T.reshape(-1).astype(np.int64)


def striped8(idx):
    return np.concatenate([x.reshape(-1, 16).T for x in idx]).astype(np.uint16)


def runs(offs, k):
    lists = np.stack([offs[16 * r : 16 * r + 16].T.reshape(-1) for r in range(8)]).astype(np.int64)
    return lists[np.arange(k) % 512 // 64]


def pack_weight(w):
    k, n = w.shape
    w = f64(np.asarray(w, np.float32).astype(ml_dtypes.bfloat16)).reshape(k // 32, 32, n)
    amax = np.abs(w).max(1)
    byte = np.clip(np.where(amax > 0, np.frexp(amax)[1] - 1 + 127 - 7, 1), 1, 254)
    scaled = (w * np.exp2(127.0 - byte)[:, None, :]).reshape(k, n).astype(np.float32)
    words = np.ascontiguousarray(scaled.reshape(k // 512, 128, 4, n).transpose(0, 1, 3, 2)).astype(ml_dtypes.float8_e4m3fn).view(np.uint8)
    return words, np.ascontiguousarray(byte.astype(np.uint8).reshape(k // 512, 16, n))


def unpack_weight(words, scales):
    g, p, n, _ = words.shape
    vals = np.ascontiguousarray(words).view(ml_dtypes.float8_e4m3fn).astype(np.float64) * np.repeat(np.exp2(scales.astype(np.float64) - 127.0), 8, axis=1)[..., None]
    return vals.transpose(0, 1, 3, 2).reshape(g * 512, n)


K, T, S, H, J, G = 512, 2048, 512, 512, 512, 2048


def setup_inputs():
    n = np.random.standard_normal
    s = mx_kscale(K)[:, None]
    packed_xT = pack_weight(n((K, T)) * s)
    packed_dT = pack_weight(n((K, G)) / s)
    return {
        "x_words": packed_xT[0],
        "x_scales": packed_xT[1],
        "w1": (n((K, H)) / np.sqrt(K) / s).astype(np.float32),
        "tab": n((H, J)).astype(np.float32),
        "gs": (np.random.uniform(0.5, 1.5, (K, 1)) * s).astype(np.float32),
        "d_words": packed_dT[0],
        "d_scales": packed_dT[1],
        "offs": striped(np.random.permutation(T)[:S]),
        "n1": striped8(np.random.randint(0, J, (8, S))),
        "n2": striped8(np.stack([np.random.permutation(S) for _ in range(8)])),
        "k1": striped8(np.random.randint(0, G, (8, H))),
        "n3": striped8(np.stack([np.random.permutation(S) for _ in range(8)])),
    }


def reference(x_words, x_scales, w1, tab, gs, d_words, d_scales, offs, n1, n2, k1, n3):
    d_k1 = unpack_weight(d_words, d_scales)[np.arange(K)[:, None], runs(k1, K)]
    xq = unpack_weight(x_words, x_scales)[:, unstriped(offs)]
    y = mxq(f64(w1), 0, "e4m3").T @ xq
    z = f64(gs) * (np.abs(y - (y[np.arange(H)[:, None], runs(n2, H)]) - (f64(tab)[np.arange(H)[:, None], runs(n1, H)])))
    h = 0.0625 * ((d_k1.T @ mxq(z, 0, "e4m3")))
    return h / (np.abs(h[np.arange(H)[:, None], runs(n3, H)]) + 0.5)

@@ -1,0 +1,203 @@
+from contextlib import ExitStack
+
+import concourse.mybir as mybir
+
+F32 = mybir.dt.float32
+BF16 = mybir.dt.bfloat16
+I32 = mybir.dt.int32
+U32 = mybir.dt.uint32
+U16 = mybir.dt.uint16
+U8 = mybir.dt.uint8
+FP8X4 = mybir.dt.float8_e4m3fn_x4
+ACT = mybir.ActivationFunctionType
+ALU = mybir.AluOpType
+
+P = 128
+PACK = 4
+S = 512
+T = 2048
+HALF = 256
+FLOPS = 2 * 2 * 512 * 512 * 512
+PRE = (0,)
+
+
+def tile_picked_densekinddnorm_none_p_kernel(
+    tc, x_words, x_scales, w1, tab, gs, d_words, d_scales, offs, n1, n2, k1, n3, out
+):
+    nc = tc.nc
+    with ExitStack() as ctx:
+        keep = ctx.enter_context(tc.tile_pool(name="keep", bufs=1))
+        psum = ctx.enter_context(tc.psum_pool(name="psum", bufs=1))
+
+        def sb(name, shape, dtype):
+            return keep.tile(shape, dtype, name=name, align_bytes=64)
+
+        lists = {}
+        for name in ("offs", "n1", "n2", "k1", "n3"):
+            lists[name] = keep.tile([P, S // 16], U16, name="list_" + name)
+
+        def half_of(name, h):
+            return lists[name][:, h * (HALF // 16) : (h + 1) * (HALF // 16)]
+
+        xs = sb("xs", [P, T], U8)
+        ds = sb("ds", [P, T], U8)
+        db = sb("db", [P, S], U8)
+        warm = sb("warm", [P, 1], F32)
+        warm_out = sb("warm_out", [P, 1], F32)
+        nc.gpsimd.memset(xs[:].bitcast(I32), 0)
+        nc.vector.memset(warm[:], 1.0)
+        nc.vector.memset(ds[:].bitcast(I32), 0)
+        nc.gpsimd.memset(db[:].bitcast(I32), 0)
+
+        xw = sb("xw", [P, T], U32)
+        dw = sb("dw", [P, T], U32)
+        w_raw = sb("w_raw", [P, PACK, S], F32)
+        tabs = [sb("tab%d" % t, [P, S], F32) for t in range(PACK)]
+        gain = sb("gain", [P, PACK], F32)
+
+        w_rows = w1.rearrange("(p j) c -> p j c", j=PACK)
+        tab_rows = tab.rearrange("(p t) c -> p t c", t=PACK)
+        x_rows = x_scales[0].bitcast(I32)
+        d_rows = d_scales[0].bitcast(I32)
+
+        nc.sync.dma_start(lists["offs"][:], offs)
+        nc.sync.dma_start(lists["k1"][:], k1)
+        nc.sync.dma_start(w_raw[:], w_rows)
+        for q in range(4):
+            nc.scalar.dma_start(xs[32 * q : 32 * q + 4, :].bitcast(I32), x_rows[4 * q : 4 * q + 4, :])
+        nc.scalar.dma_start(ds[0:P:8, :].bitcast(I32), d_rows)
+        nc.scalar.activation(warm_out[:], warm[:], ACT.Abs_reciprocal_sqrt)
+        nc.sync.dma_start(xw[:].bitcast(I32), x_words[0].rearrange("p n t -> p (n t)").bitcast(I32))
+        nc.sync.dma_start(lists["n1"][:], n1)
+        nc.sync.dma_start(tabs[0][:], tab_rows[:, 0, :])
+        nc.sync.dma_start(lists["n2"][:], n2)
+        nc.sync.dma_start(gain[:], gs.rearrange("(p t) o -> p (t o)", t=PACK))
+        for t in range(1, PACK):
+            nc.sync.dma_start(tabs[t][:], tab_rows[:, t, :])
+        nc.sync.dma_start(dw[:].bitcast(I32), d_words[0].rearrange("p n t -> p (n t)").bitcast(I32))
+        nc.sync.dma_start(lists["n3"][:], n3)
+
+        wb = sb("wb", [P, PACK * S], BF16)
+        wb_view = wb[:].rearrange("p (t m j) -> p m j t", t=PACK, j=PACK)
+        w_view = w_raw[:].rearrange("p j (m t) -> p m j t", t=PACK)
+        nc.scalar.copy(wb_view[:, :64], w_view[:, :64])
+        nc.vector.tensor_copy(wb_view[:, 64:], w_view[:, 64:])
+
+        xgs = sb("xgs", [P, S], U8)
+        nc.vector.tensor_copy(xgs[:], xs[:].indirect(lists["offs"][:]))
+        dgs = sb("dgs", [P, S], U8)
+        nc.vector.tensor_copy(dgs[:], ds[:].indirect(lists["k1"][:]))
+        dds = sb("dds", [P, S], U8)
+        nc.vector.tensor_copy(dds[:].rearrange("p (t m) -> p t m", t=PACK), dgs[:].rearrange("p (m t) -> p t m", t=PACK))
+        for a in range(4):
+            nc.sync.dma_start(db[a:P:32, :].bitcast(I32), dds[8 * a : P : 32, :].bitcast(I32))
+
+        wq = sb("wq", [P, S], U32)
+        wqs = sb("wqs", [P, S], U8)
+        nc.vector.quantize_mx(out=wq[:].bitcast(FP8X4), scales=wqs[:], in_=wb[:])
+        xg = sb("xg", [P, S], U32)
+        nc.vector.tensor_copy(xg[:], xw[:].indirect(lists["offs"][:]))
+
+        y_ps = [psum.tile([P, S], F32, name="y_ps%d" % t, tag="bank%d" % t) for t in range(PACK)]
+        ys = [sb("y%d" % t, [P, S], F32) for t in range(PACK)]
+        for t in range(PACK):
+            cols = slice(t * P, (t + 1) * P)
+            nc.tensor.matmul_mx(
+                out=y_ps[t][:], lhsT=wq[:, cols].bitcast(FP8X4), lhsT_scale=wqs[:, cols],
+                rhs=xg[:].bitcast(FP8X4), rhs_scale=xgs[:], start=True, stop=True,
+            )
+            nc.scalar.copy(ys[t][:], y_ps[t][:])
+
+        dif = [[sb("dif%d_%d" % (t, h), [P, HALF], F32) for h in range(2)] for t in range(PACK)]
+        err = [[sb("err%d_%d" % (t, h), [P, HALF], F32) for h in range(2)] for t in range(PACK)]
+        mag = [[sb("mag%d_%d" % (t, h), [P, HALF], F32) for h in range(2)] for t in range(PACK)]
+        zb = [sb("zb%d" % h, [P, PACK, HALF], BF16) for h in range(2)]
+        zi = [sb("zi%d" % h, [P, HALF, PACK], BF16) for h in range(2)]
+        zq = [sb("zq%d" % h, [P, HALF], U32) for h in range(2)]
+        zqs = [sb("zqs%d" % h, [P, HALF], U8) for h in range(2)]
+
+        picked = {}
+        for t in PRE:
+            for h in range(2):
+                picked[t, h] = sb("picked%d_%d" % (t, h), [P, HALF], F32)
+                nc.vector.tensor_copy(picked[t, h][:], tabs[t][:].indirect(half_of("n1", h)))
+
+        def first(t, h):
+            cols = slice(h * HALF, (h + 1) * HALF)
+            if t in PRE:
+                nc.vector.tensor_tensor(dif[t][h][:], picked[t, h][:], y_ps[t][:, cols], ALU.subtract)
+            else:
+                nc.vector.tensor_tensor(dif[t][h][:], tabs[t][:].indirect(half_of("n1", h)), ys[t][:, cols], ALU.subtract)
+
+        def second(t, h):
+            nc.vector.tensor_tensor(err[t][h][:], ys[t][:].indirect(half_of("n2", h)), dif[t][h][:], ALU.add)
+            nc.scalar.activation(mag[t][h][:], err[t][h][:], ACT.Abs)
+            nc.scalar.activation(zb[h][:, t, :], mag[t][h][:], ACT.Copy, scale=gain[:, t : t + 1])
+
+        def weave(h):
+            dst = zi[h][:].rearrange("p (c i) t -> p c t i", i=4)
+            srcv = zb[h][:].rearrange("p t (c i) -> p c t i", i=4)
+            if h == 0:
+                nc.scalar.copy(dst, srcv)
+            else:
+                nc.vector.tensor_copy(dst, srcv)
+
+        def quantise(h):
+            nc.vector.quantize_mx(out=zq[h][:].bitcast(FP8X4), scales=zqs[h][:], in_=zi[h][:].rearrange("p n t -> p (n t)"))
+
+        dg = sb("dg", [P, S], U32)
+        dd = sb("dd", [P, S], U32)
+
+        steps = [(t, h) for h in range(2) for t in range(PACK)]
+        first(*steps[0])
+        for i in range(len(steps)):
+            if i + 1 < len(steps):
+                first(*steps[i + 1])
+            second(*steps[i])
+            if i == PACK - 1:
+                weave(0)
+        nc.vector.tensor_copy(dg[:], dw[:].indirect(lists["k1"][:]))
+        quantise(0)
+        nc.vector.tensor_copy(dd[:].rearrange("p (t m) -> p t m", t=PACK), dg[:].rearrange("p (m t) -> p t m", t=PACK))
+        weave(1)
+        quantise(1)
+
+        h_ps = {}
+        habs = [sb("habs%d" % t, [P, S], F32) for t in range(PACK)]
+        for h in range(2):
+            for t in range(PACK):
+                cols = slice(t * P, (t + 1) * P)
+                h_ps[t, h] = psum.tile([P, HALF], F32, name="h_ps%d_%d" % (t, h), tag="bank%d" % (t + PACK * (1 - h)))
+                nc.tensor.matmul_mx(
+                    out=h_ps[t, h][:], lhsT=dd[:, cols].bitcast(FP8X4), lhsT_scale=db[:, cols],
+                    rhs=zq[h][:].bitcast(FP8X4), rhs_scale=zqs[h][:], start=True, stop=True,
+                )
+                nc.scalar.activation(habs[t][:, h * HALF : (h + 1) * HALF], h_ps[t, h][:], ACT.Abs)
+
+        out_rows = out.rearrange("(p t) c -> p t c", t=PACK)
+        got = {}
+        for t in range(PACK):
+            for h in range(2):
+                got[t, h] = sb("got%d_%d" % (t, h), [P, HALF], F32)
+
+        def fetch(t):
+            for h in range(2):
+                nc.vector.tensor_copy(got[t, h][:], habs[t][:].indirect(half_of("n3", h)))
+                root = sb("root%d_%d" % (t, h), [P, HALF], F32)
+                nc.scalar.activation(root[:], got[t, h][:], ACT.Abs_reciprocal_sqrt, bias=8.0)
+                nc.scalar.activation(got[t, h][:], root[:], ACT.Square)
+
+        def finish(t):
+            res = sb("res%d" % t, [P, S], F32)
+            for h in range(2):
+                cols = slice(h * HALF, (h + 1) * HALF)
+                nc.vector.tensor_tensor(res[:, cols], h_ps[t, h][:], got[t, h][:], ALU.mult)
+            nc.sync.dma_start(out_rows[:, t, :], res[:])
+
+        fetch(0)
+        fetch(1)
+        fetch(2)
+        finish(0)
+        fetch(3)
+        for t in range(1, PACK):
+            finish(t)

@@ -18,7 +18,7 @@ S = 512
 T = 2048
 HALF = 256
 FLOPS = 2 * 2 * 512 * 512 * 512
-PRE = (0,)
+PRE = ()
 
 
 def tile_picked_densekinddnorm_none_p_kernel(
@@ -44,10 +44,8 @@ def tile_picked_densekinddnorm_none_p_kernel(
         db = sb("db", [P, S], U8)
         warm = sb("warm", [P, 1], F32)
         warm_out = sb("warm_out", [P, 1], F32)
-        nc.gpsimd.memset(xs[:].bitcast(I32), 0)
         nc.vector.memset(warm[:], 1.0)
-        nc.vector.memset(ds[:].bitcast(I32), 0)
-        nc.gpsimd.memset(db[:].bitcast(I32), 0)
+        nc.vector.memset(db[:].bitcast(I32), 0)
 
         xw = sb("xw", [P, T], U32)
         dw = sb("dw", [P, T], U32)
@@ -61,21 +59,24 @@ def tile_picked_densekinddnorm_none_p_kernel(
         d_rows = d_scales[0].bitcast(I32)
 
         nc.sync.dma_start(lists["offs"][:], offs)
-        nc.sync.dma_start(lists["k1"][:], k1)
-        nc.sync.dma_start(w_raw[:], w_rows)
         for q in range(4):
-            nc.scalar.dma_start(xs[32 * q : 32 * q + 4, :].bitcast(I32), x_rows[4 * q : 4 * q + 4, :])
-        nc.scalar.dma_start(ds[0:P:8, :].bitcast(I32), d_rows)
-        nc.scalar.activation(warm_out[:], warm[:], ACT.Abs_reciprocal_sqrt)
+            nc.sync.dma_start(
+                xs[32 * q : 32 * q + 32, :].bitcast(I32),
+                x_rows[4 * q : 4 * q + 4, :].unsqueeze(0).to_broadcast([8, 4, T // 4]),
+            )
+        nc.sync.dma_start(w_raw[:], w_rows)
         nc.sync.dma_start(xw[:].bitcast(I32), x_words[0].rearrange("p n t -> p (n t)").bitcast(I32))
+        nc.sync.dma_start(lists["k1"][:], k1)
+        nc.sync.dma_start(ds[:].bitcast(I32), d_rows.unsqueeze(1).to_broadcast([16, 8, T // 4]))
+        nc.scalar.activation(warm_out[:], warm[:], ACT.Abs_reciprocal_sqrt)
         nc.sync.dma_start(lists["n1"][:], n1)
         nc.sync.dma_start(tabs[0][:], tab_rows[:, 0, :])
         nc.sync.dma_start(lists["n2"][:], n2)
         nc.sync.dma_start(gain[:], gs.rearrange("(p t) o -> p (t o)", t=PACK))
         for t in range(1, PACK):
             nc.sync.dma_start(tabs[t][:], tab_rows[:, t, :])
-        nc.sync.dma_start(dw[:].bitcast(I32), d_words[0].rearrange("p n t -> p (n t)").bitcast(I32))
         nc.sync.dma_start(lists["n3"][:], n3)
+        nc.sync.dma_start(dw[:].bitcast(I32), d_words[0].rearrange("p n t -> p (n t)").bitcast(I32))
 
         wb = sb("wb", [P, PACK * S], BF16)
         wb_view = wb[:].rearrange("p (t m j) -> p m j t", t=PACK, j=PACK)
@@ -85,18 +86,19 @@ def tile_picked_densekinddnorm_none_p_kernel(
 
         xgs = sb("xgs", [P, S], U8)
         nc.vector.tensor_copy(xgs[:], xs[:].indirect(lists["offs"][:]))
-        dgs = sb("dgs", [P, S], U8)
-        nc.vector.tensor_copy(dgs[:], ds[:].indirect(lists["k1"][:]))
-        dds = sb("dds", [P, S], U8)
-        nc.vector.tensor_copy(dds[:].rearrange("p (t m) -> p t m", t=PACK), dgs[:].rearrange("p (m t) -> p t m", t=PACK))
-        for a in range(4):
-            nc.sync.dma_start(db[a:P:32, :].bitcast(I32), dds[8 * a : P : 32, :].bitcast(I32))
 
         wq = sb("wq", [P, S], U32)
         wqs = sb("wqs", [P, S], U8)
         nc.vector.quantize_mx(out=wq[:].bitcast(FP8X4), scales=wqs[:], in_=wb[:])
         xg = sb("xg", [P, S], U32)
         nc.vector.tensor_copy(xg[:], xw[:].indirect(lists["offs"][:]))
+
+        dgs = sb("dgs", [P, S], U8)
+        nc.vector.tensor_copy(dgs[:], ds[:].indirect(lists["k1"][:]))
+        dds = sb("dds", [P, S], U8)
+        nc.vector.tensor_copy(dds[:].rearrange("p (t m) -> p t m", t=PACK), dgs[:].rearrange("p (m t) -> p t m", t=PACK))
+        for a in range(4):
+            nc.sync.dma_start(db[a:P:32, :].bitcast(I32), dds[8 * a : P : 32, :].bitcast(I32))
 
         y_ps = [psum.tile([P, S], F32, name="y_ps%d" % t, tag="bank%d" % t) for t in range(PACK)]
         ys = [sb("y%d" % t, [P, S], F32) for t in range(PACK)]
@@ -175,29 +177,20 @@ def tile_picked_densekinddnorm_none_p_kernel(
                 nc.scalar.activation(habs[t][:, h * HALF : (h + 1) * HALF], h_ps[t, h][:], ACT.Abs)
 
         out_rows = out.rearrange("(p t) c -> p t c", t=PACK)
-        got = {}
+        got = [sb("got%d" % t, [P, S], F32) for t in range(PACK)]
+        inv = [sb("inv%d" % t, [P, S], F32) for t in range(PACK)]
         for t in range(PACK):
             for h in range(2):
-                got[t, h] = sb("got%d_%d" % (t, h), [P, HALF], F32)
-
-        def fetch(t):
-            for h in range(2):
-                nc.vector.tensor_copy(got[t, h][:], habs[t][:].indirect(half_of("n3", h)))
-                root = sb("root%d_%d" % (t, h), [P, HALF], F32)
-                nc.scalar.activation(root[:], got[t, h][:], ACT.Abs_reciprocal_sqrt, bias=8.0)
-                nc.scalar.activation(got[t, h][:], root[:], ACT.Square)
-
-        def finish(t):
+                nc.vector.tensor_copy(got[t][:, h * HALF : (h + 1) * HALF], habs[t][:].indirect(half_of("n3", h)))
+            root = sb("root%d" % t, [P, S], F32)
+            nc.scalar.activation(root[:], got[t][:], ACT.Abs_reciprocal_sqrt, bias=8.0)
+            nc.scalar.activation(inv[t][:], root[:], ACT.Square)
+        for t in range(PACK):
             res = sb("res%d" % t, [P, S], F32)
             for h in range(2):
                 cols = slice(h * HALF, (h + 1) * HALF)
-                nc.vector.tensor_tensor(res[:, cols], h_ps[t, h][:], got[t, h][:], ALU.mult)
-            nc.sync.dma_start(out_rows[:, t, :], res[:])
-
-        fetch(0)
-        fetch(1)
-        fetch(2)
-        finish(0)
-        fetch(3)
-        for t in range(1, PACK):
-            finish(t)
+                nc.vector.tensor_tensor(res[:, cols], h_ps[t, h][:], inv[t][:, cols], ALU.mult)
+                if t == PACK - 1:
+                    nc.sync.dma_start(out_rows[:, t, cols], res[:, cols])
+            if t < PACK - 1:
+                nc.sync.dma_start(out_rows[:, t, :], res[:])

from contextlib import ExitStack

import concourse.mybir as mybir

F32 = mybir.dt.float32
BF16 = mybir.dt.bfloat16
I32 = mybir.dt.int32
U32 = mybir.dt.uint32
U16 = mybir.dt.uint16
U8 = mybir.dt.uint8
FP8X4 = mybir.dt.float8_e4m3fn_x4
ACT = mybir.ActivationFunctionType
ALU = mybir.AluOpType

P = 128
PACK = 4
S = 512
T = 2048
HALF = 256
FLOPS = 2 * 2 * 512 * 512 * 512
PRE = ()


def tile_picked_densekinddnorm_none_p_kernel(
    tc, x_words, x_scales, w1, tab, gs, d_words, d_scales, offs, n1, n2, k1, n3, out
):
    nc = tc.nc
    with ExitStack() as ctx:
        keep = ctx.enter_context(tc.tile_pool(name="keep", bufs=1))
        psum = ctx.enter_context(tc.psum_pool(name="psum", bufs=1))

        def sb(name, shape, dtype):
            return keep.tile(shape, dtype, name=name, align_bytes=64)

        lists = {}
        for name in ("offs", "n1", "n2", "k1", "n3"):
            lists[name] = keep.tile([P, S // 16], U16, name="list_" + name)

        def half_of(name, h):
            return lists[name][:, h * (HALF // 16) : (h + 1) * (HALF // 16)]

        xs = sb("xs", [P, T], U8)
        ds = sb("ds", [P, T], U8)
        db = sb("db", [P, S], U8)
        warm = sb("warm", [P, 1], F32)
        warm_out = sb("warm_out", [P, 1], F32)
        nc.vector.memset(warm[:], 1.0)
        nc.vector.memset(db[:].bitcast(I32), 0)

        xw = sb("xw", [P, T], U32)
        dw = sb("dw", [P, T], U32)
        w_raw = sb("w_raw", [P, PACK, S], F32)
        tabs = [sb("tab%d" % t, [P, S], F32) for t in range(PACK)]
        gain = sb("gain", [P, PACK], F32)

        w_rows = w1.rearrange("(p j) c -> p j c", j=PACK)
        tab_rows = tab.rearrange("(p t) c -> p t c", t=PACK)
        x_rows = x_scales[0].bitcast(I32)
        d_rows = d_scales[0].bitcast(I32)

        nc.sync.dma_start(lists["offs"][:], offs)
        for q in range(4):
            nc.sync.dma_start(
                xs[32 * q : 32 * q + 32, :].bitcast(I32),
                x_rows[4 * q : 4 * q + 4, :].unsqueeze(0).to_broadcast([8, 4, T // 4]),
            )
        nc.sync.dma_start(w_raw[:], w_rows)
        nc.sync.dma_start(xw[:].bitcast(I32), x_words[0].rearrange("p n t -> p (n t)").bitcast(I32))
        nc.sync.dma_start(lists["k1"][:], k1)
        nc.sync.dma_start(ds[:].bitcast(I32), d_rows.unsqueeze(1).to_broadcast([16, 8, T // 4]))
        nc.scalar.activation(warm_out[:], warm[:], ACT.Abs_reciprocal_sqrt)
        nc.sync.dma_start(lists["n1"][:], n1)
        nc.sync.dma_start(tabs[0][:], tab_rows[:, 0, :])
        nc.sync.dma_start(lists["n2"][:], n2)
        nc.sync.dma_start(gain[:], gs.rearrange("(p t) o -> p (t o)", t=PACK))
        for t in range(1, PACK):
            nc.sync.dma_start(tabs[t][:], tab_rows[:, t, :])
        nc.sync.dma_start(lists["n3"][:], n3)
        nc.sync.dma_start(dw[:].bitcast(I32), d_words[0].rearrange("p n t -> p (n t)").bitcast(I32))

        wb = sb("wb", [P, PACK * S], BF16)
        wb_view = wb[:].rearrange("p (t m j) -> p m j t", t=PACK, j=PACK)
        w_view = w_raw[:].rearrange("p j (m t) -> p m j t", t=PACK)
        nc.scalar.copy(wb_view[:, :64], w_view[:, :64])
        nc.vector.tensor_copy(wb_view[:, 64:], w_view[:, 64:])

        xgs = sb("xgs", [P, S], U8)
        nc.vector.tensor_copy(xgs[:], xs[:].indirect(lists["offs"][:]))

        wq = sb("wq", [P, S], U32)
        wqs = sb("wqs", [P, S], U8)
        nc.vector.quantize_mx(out=wq[:].bitcast(FP8X4), scales=wqs[:], in_=wb[:])
        xg = sb("xg", [P, S], U32)
        nc.vector.tensor_copy(xg[:], xw[:].indirect(lists["offs"][:]))

        dgs = sb("dgs", [P, S], U8)
        nc.vector.tensor_copy(dgs[:], ds[:].indirect(lists["k1"][:]))
        dds = sb("dds", [P, S], U8)
        nc.vector.tensor_copy(dds[:].rearrange("p (t m) -> p t m", t=PACK), dgs[:].rearrange("p (m t) -> p t m", t=PACK))
        for a in range(4):
            nc.sync.dma_start(db[a:P:32, :].bitcast(I32), dds[8 * a : P : 32, :].bitcast(I32))

        y_ps = [psum.tile([P, S], F32, name="y_ps%d" % t, tag="bank%d" % t) for t in range(PACK)]
        ys = [sb("y%d" % t, [P, S], F32) for t in range(PACK)]
        for t in range(PACK):
            cols = slice(t * P, (t + 1) * P)
            nc.tensor.matmul_mx(
                out=y_ps[t][:], lhsT=wq[:, cols].bitcast(FP8X4), lhsT_scale=wqs[:, cols],
                rhs=xg[:].bitcast(FP8X4), rhs_scale=xgs[:], start=True, stop=True,
            )
            nc.scalar.copy(ys[t][:], y_ps[t][:])

        dif = [[sb("dif%d_%d" % (t, h), [P, HALF], F32) for h in range(2)] for t in range(PACK)]
        err = [[sb("err%d_%d" % (t, h), [P, HALF], F32) for h in range(2)] for t in range(PACK)]
        mag = [[sb("mag%d_%d" % (t, h), [P, HALF], F32) for h in range(2)] for t in range(PACK)]
        zb = [sb("zb%d" % h, [P, PACK, HALF], BF16) for h in range(2)]
        zi = [sb("zi%d" % h, [P, HALF, PACK], BF16) for h in range(2)]
        zq = [sb("zq%d" % h, [P, HALF], U32) for h in range(2)]
        zqs = [sb("zqs%d" % h, [P, HALF], U8) for h in range(2)]

        picked = {}
        for t in PRE:
            for h in range(2):
                picked[t, h] = sb("picked%d_%d" % (t, h), [P, HALF], F32)
                nc.vector.tensor_copy(picked[t, h][:], tabs[t][:].indirect(half_of("n1", h)))

        def first(t, h):
            cols = slice(h * HALF, (h + 1) * HALF)
            if t in PRE:
                nc.vector.tensor_tensor(dif[t][h][:], picked[t, h][:], y_ps[t][:, cols], ALU.subtract)
            else:
                nc.vector.tensor_tensor(dif[t][h][:], tabs[t][:].indirect(half_of("n1", h)), ys[t][:, cols], ALU.subtract)

        def second(t, h):
            nc.vector.tensor_tensor(err[t][h][:], ys[t][:].indirect(half_of("n2", h)), dif[t][h][:], ALU.add)
            nc.scalar.activation(mag[t][h][:], err[t][h][:], ACT.Abs)
            nc.scalar.activation(zb[h][:, t, :], mag[t][h][:], ACT.Copy, scale=gain[:, t : t + 1])

        def weave(h):
            dst = zi[h][:].rearrange("p (c i) t -> p c t i", i=4)
            srcv = zb[h][:].rearrange("p t (c i) -> p c t i", i=4)
            if h == 0:
                nc.scalar.copy(dst, srcv)
            else:
                nc.vector.tensor_copy(dst, srcv)

        def quantise(h):
            nc.vector.quantize_mx(out=zq[h][:].bitcast(FP8X4), scales=zqs[h][:], in_=zi[h][:].rearrange("p n t -> p (n t)"))

        dg = sb("dg", [P, S], U32)
        dd = sb("dd", [P, S], U32)

        steps = [(t, h) for h in range(2) for t in range(PACK)]
        first(*steps[0])
        for i in range(len(steps)):
            if i + 1 < len(steps):
                first(*steps[i + 1])
            second(*steps[i])
            if i == PACK - 1:
                weave(0)
        nc.vector.tensor_copy(dg[:], dw[:].indirect(lists["k1"][:]))
        quantise(0)
        nc.vector.tensor_copy(dd[:].rearrange("p (t m) -> p t m", t=PACK), dg[:].rearrange("p (m t) -> p t m", t=PACK))
        weave(1)
        quantise(1)

        h_ps = {}
        habs = [sb("habs%d" % t, [P, S], F32) for t in range(PACK)]
        for h in range(2):
            for t in range(PACK):
                cols = slice(t * P, (t + 1) * P)
                h_ps[t, h] = psum.tile([P, HALF], F32, name="h_ps%d_%d" % (t, h), tag="bank%d" % (t + PACK * (1 - h)))
                nc.tensor.matmul_mx(
                    out=h_ps[t, h][:], lhsT=dd[:, cols].bitcast(FP8X4), lhsT_scale=db[:, cols],
                    rhs=zq[h][:].bitcast(FP8X4), rhs_scale=zqs[h][:], start=True, stop=True,
                )
                nc.scalar.activation(habs[t][:, h * HALF : (h + 1) * HALF], h_ps[t, h][:], ACT.Abs)

        out_rows = out.rearrange("(p t) c -> p t c", t=PACK)
        got = [sb("got%d" % t, [P, S], F32) for t in range(PACK)]
        inv = [sb("inv%d" % t, [P, S], F32) for t in range(PACK)]
        for t in range(PACK):
            for h in range(2):
                nc.vector.tensor_copy(got[t][:, h * HALF : (h + 1) * HALF], habs[t][:].indirect(half_of("n3", h)))
            root = sb("root%d" % t, [P, S], F32)
            nc.scalar.activation(root[:], got[t][:], ACT.Abs_reciprocal_sqrt, bias=8.0)
            nc.scalar.activation(inv[t][:], root[:], ACT.Square)
        for t in range(PACK):
            res = sb("res%d" % t, [P, S], F32)
            for h in range(2):
                cols = slice(h * HALF, (h + 1) * HALF)
                nc.vector.tensor_tensor(res[:, cols], h_ps[t, h][:], inv[t][:, cols], ALU.mult)
                if t == PACK - 1:
                    nc.sync.dma_start(out_rows[:, t, cols], res[:, cols])
            if t < PACK - 1:
                nc.sync.dma_start(out_rows[:, t, :], res[:])
